import numpy as np
import ml_dtypes


def mxq(x, axis, fmt="e4m3"):
    dtype, down = {"e4m3": (ml_dtypes.float8_e4m3fn, 7), "e5m2": (ml_dtypes.float8_e5m2, 14)}[fmt]
    v = np.moveaxis(np.asarray(x, np.float32).astype(ml_dtypes.bfloat16).astype(np.float64), axis, -1)
    blocks = v.reshape(v.shape[:-1] + (-1, 32))
    amax = np.abs(blocks).max(-1, keepdims=True)
    byte = np.maximum(np.where(amax > 0, np.frexp(amax)[1] - 1 + 127, 0) - down, 1)
    scale = np.exp2(byte - 127.0)
    codes = (blocks / scale).astype(np.float32).astype(dtype).astype(np.float64)
    return np.moveaxis((codes * scale).reshape(v.shape), -1, axis)


WIDE = False


def mx_kscale(k):
    if not WIDE:
        return np.ones(k)
    levels = np.array([10, -10, 5, -5, 0])
    if k % 512:
        return np.exp2(np.random.permutation(np.resize(levels, k // 32))).repeat(32)
    a = np.empty((k // 512, 16))
    for p in range(k // 512):
        a[p, :8] = np.random.permutation(np.resize(levels, 8))
        for g in range(8):
            far = levels[np.abs(levels - a[p, g]) >= 10]
            a[p, g + 8] = far[np.random.randint(len(far))]
    return np.exp2(a.ravel()).repeat(32)


def f64(x):
    return np.asarray(x).astype(np.float64)


def striped(idx):
    return np.tile(np.asarray(idx).reshape(-1, 16).T, (8, 1)).astype(np.uint16)


def unstriped(offs):
    return offs[:16].T.reshape(-1).astype(np.int64)


E2M1 = np.array([0.0, 0.5, 1.0, 1.5, 2.0, 3.0, 4.0, 6.0, -0.0, -0.5, -1.0, -1.5, -2.0, -3.0, -4.0, -6.0])


def pack_weight(w, fmt):
    k, n = w.shape
    w = f64(np.asarray(w, np.float32).astype(ml_dtypes.bfloat16)).reshape(k // 32, 32, n)
    amax = np.abs(w).max(1)
    if fmt == "e4m3":
        byte = np.frexp(amax)[1] - 1 + 127 - 7
    else:
        mant, ex = np.frexp(amax / 6.0)
        byte = np.where(mant > 0.5, ex, ex - 1) + 127
    byte = np.clip(np.where(amax > 0, byte, 1), 1, 254)
    scaled = (w * np.exp2(127.0 - byte)[:, None, :]).reshape(k, n).astype(np.float32)
    by_word = np.ascontiguousarray(scaled.reshape(k // 512, 128, 4, n).transpose(0, 1, 3, 2))
    if fmt == "e4m3":
        words = by_word.astype(ml_dtypes.float8_e4m3fn).view(np.uint8)
    else:
        c = by_word.astype(ml_dtypes.float4_e2m1fn).view(np.uint8) & 0xF
        words = (c[..., 0::2] | (c[..., 1::2] << 4)).reshape(k // 512, 128, 2 * n)
    return np.ascontiguousarray(words), np.ascontiguousarray(byte.astype(np.uint8).reshape(k // 512, 16, n))


def unpack_weight(words, scales, fmt):
    g, _, n = scales.shape
    words = np.ascontiguousarray(words).reshape(g, 128, n, -1)
    if fmt == "e4m3":
        vals = words.view(ml_dtypes.float8_e4m3fn).astype(np.float64)
    else:
        nib = np.empty((g, 128, n, 4), np.uint8)
        nib[..., 0::2] = words & 0xF
        nib[..., 1::2] = words >> 4
        vals = E2M1[nib]
    vals = vals * np.repeat(np.exp2(scales.astype(np.float64) - 127.0), 8, axis=1)[..., None]
    return vals.transpose(0, 1, 3, 2).reshape(g * 512, n)


D, T, I, Q, V, G, M = 512, 2048, 512, 128, 16, 64, 512


def setup_inputs():
    n = np.random.standard_normal
    idx = np.random.permutation(T)[:I]
    idx2 = np.random.permutation(M)[:G]
    fd = mx_kscale(D)
    keysp = pack_weight(n((D, T)) / fd[:, None], "e4m3")
    return {
        "query": (n((D, Q)) * 1.0 / np.sqrt(D) * fd[:, None]).astype(np.float32),
        "keys_words": keysp[0],
        "keys_scales": keysp[1],
        "lam": (np.random.uniform(0.3, 0.8, (1, Q))).astype(np.float32),
        "wear": (np.random.uniform(0.0, 3.0, (Q, T))).astype(np.float32),
        "weary": (np.random.uniform(0.4, 1.5, (Q, 1))).astype(np.float32),
        "worth": np.tile(np.random.uniform(0.2, 2.0, T), (128, 1)).astype(np.float32),
        "old": (1.0 * n((Q, M))).astype(np.float32),
        "offs": striped(idx),
        "offs2": striped(idx2),
    }


def reference(query, keys_words, keys_scales, lam, wear, weary, worth, old, offs, offs2):
    idx = unstriped(offs)
    idx2 = unstriped(offs2)
    keysu = unpack_weight(keys_words, keys_scales, "e4m3")
    keysidxg = keysu[:, idx]
    queryq = mxq(f64(query), 0, "e4m3")
    a0 = keysidxg.T @ queryq
    ag = a0.reshape(I, V, Q // V).max(axis=2)
    ar = np.repeat(ag, Q // V, axis=1)
    s0 = a0 - ar * f64(lam)
    s = s0.T
    p = np.exp(s) / (f64(wear)[:, idx] * f64(weary) + 1.0)
    w = p / np.sum(p, axis=1, keepdims=True)
    ws = w * f64(worth)[:1][:, idx] * 512.0
    wp = ws.reshape(Q, G, I // G).sum(axis=2)
    wf = np.zeros((Q, M))
    wf[:, idx2] = wp
    y = f64(old) + wf
    return y

@@ -1,0 +1,225 @@
+from contextlib import ExitStack
+
+import concourse.mybir as mybir
+from concourse.masks import make_identity
+
+D, T, SLOTS, Q, GROUP, RUN, RUNS, M = 512, 2048, 512, 128, 8, 8, 64, 512
+FLOPS = 2 * D * SLOTS * Q
+BYTES = 4 * (D * Q + 128 * T + 4 * T + Q + Q * T + Q + T + 2 * Q * M) + 2 * 128 * (32 + 4)
+
+F32 = mybir.dt.float32
+BF16 = mybir.dt.bfloat16
+I32 = mybir.dt.int32
+U32 = mybir.dt.uint32
+U16 = mybir.dt.uint16
+U8 = mybir.dt.uint8
+FP8X4 = mybir.dt.float8_e4m3fn_x4
+ALU = mybir.AluOpType
+ACT = mybir.ActivationFunctionType
+AX = mybir.AxisListType
+
+P = 128
+PACK = 4
+HALVES = 2
+HALF = SLOTS // HALVES
+CHUNKS = HALF // P
+LANES = 16
+
+
+def tile_attend_groupbest_wornout_pagesums_kernel(
+    tc, query, keys_words, keys_scales, lam, wear, weary, worth, old, offs, offs2, out
+):
+    nc = tc.nc
+    with ExitStack() as ctx:
+        keep = ctx.enter_context(tc.tile_pool(name="keep", bufs=1))
+        psum = ctx.enter_context(tc.psum_pool(name="psum", bufs=1))
+
+        def half_cols(h, width=HALF):
+            return slice(h * width, (h + 1) * width)
+
+        slot_list = keep.tile([P, SLOTS // LANES], U16, name="slot_list")
+        nc.sync.dma_start(slot_list[:], offs)
+
+        def half_list(h):
+            return slot_list[:, half_cols(h, HALF // LANES)]
+
+        scale_pool = keep.tile([P, T], U8, name="scale_pool")
+        nc.gpsimd.memset(scale_pool[:].bitcast(I32), 0)
+        for quad in range(4):
+            nc.scalar.dma_start(
+                scale_pool[32 * quad : 32 * quad + 4, :].bitcast(I32),
+                keys_scales[0, 4 * quad : 4 * quad + 4, :].bitcast(I32),
+            )
+
+        ident = keep.tile([P, P], F32, name="ident")
+        make_identity(nc, ident[:])
+        lam_col = keep.tile([P, 1], F32, name="lam_col")
+        with nc.allow_non_contiguous_dma(reason="one value a partition"):
+            nc.gpsimd.dma_start(lam_col[:], lam.rearrange("o q -> q o"))
+        weary_col = keep.tile([P, 1], F32, name="weary_col")
+        nc.gpsimd.dma_start(weary_col[:], weary)
+
+        query_raw = keep.tile([P, PACK, Q], F32, name="query_raw", tag="query_then_wear")
+        nc.sync.dma_start(query_raw[:], query.rearrange("(p j) q -> p j q", j=PACK))
+        word_pool = keep.tile([P, T], I32, name="word_pool", tag="words_then_old")
+        nc.sync.dma_start(word_pool[:], keys_words[0].rearrange("p t r -> p (t r)").bitcast(I32))
+
+        worth_pool = keep.tile([P, T], F32, name="worth_pool")
+        nc.vector.memset(worth_pool[:].bitcast(I32), 0)
+        nc.sync.dma_start(worth_pool[0:1, :], worth[0:1, :])
+        placed = keep.tile([P, M], F32, name="placed")
+        nc.vector.memset(placed[:].bitcast(I32), 0)
+
+        query_bf = keep.tile([P, Q, PACK], BF16, name="query_bf", align_bytes=64)
+        nc.vector.tensor_copy(query_bf[:], query_raw[:].rearrange("p j q -> p q j"))
+        query_words = keep.tile([P, Q], U32, name="query_words", align_bytes=64)
+        query_scales = keep.tile([P, Q], U8, name="query_scales", align_bytes=64)
+        nc.vector.quantize_mx(
+            out=query_words[:].bitcast(FP8X4),
+            scales=query_scales[:],
+            in_=query_bf[:].rearrange("p q j -> p (q j)"),
+        )
+
+        wear_pool = keep.tile([P, T], F32, name="wear_pool", tag="query_then_wear")
+        nc.sync.dma_start(wear_pool[:], wear)
+        run_list = keep.tile([P, RUNS // LANES], U16, name="run_list")
+        nc.sync.dma_start(run_list[:], offs2)
+
+        key_scales = keep.tile([P, SLOTS], U8, name="key_scales", align_bytes=64)
+        nc.vector.tensor_copy(key_scales[:], scale_pool[:].indirect(slot_list[:]))
+
+        worth_listed = keep.tile([P, SLOTS], F32, name="worth_listed", tag="worth_then_raw")
+        nc.scalar.activation(worth_listed[:], worth_pool[:].indirect(slot_list[:]), ACT.Copy)
+        turned = psum.tile([P, SLOTS // P, P], F32, name="turned", tag="turned_then_raw")
+        for c in range(SLOTS // P):
+            nc.tensor.transpose(turned[:, c, :], worth_listed[:, c * P : (c + 1) * P], ident[:])
+        worth_cols = keep.tile([P, SLOTS // P], F32, name="worth_cols")
+        nc.scalar.copy(worth_cols[:], turned[:, :, 0])
+
+        lam_row = psum.tile([P, Q], F32, name="lam_row")
+        nc.tensor.transpose(lam_row[:], lam_col[:].to_broadcast([P, P]), ident[:])
+
+        key_words, raw_psum = [], []
+        for h in range(HALVES):
+            words = keep.tile([P, HALF], U32, name="key_words%d" % h, tag="words%d" % h, align_bytes=64)
+            nc.vector.tensor_copy(words[:], word_pool[:].bitcast(U32).indirect(half_list(h)))
+            key_words.append(words)
+            raw = psum.tile([P, CHUNKS, Q], F32, name="raw%d" % h, tag=("raw_then_worth", "turned_then_raw")[h])
+            for c in range(CHUNKS):
+                first = h * HALF + c * P
+                nc.tensor.matmul_mx(
+                    out=raw[:, c, :],
+                    lhsT=words[:, c * P : (c + 1) * P].bitcast(FP8X4),
+                    lhsT_scale=key_scales[:, first : first + P],
+                    rhs=query_words[:].bitcast(FP8X4),
+                    rhs_scale=query_scales[:],
+                    start=True,
+                    stop=True,
+                )
+            raw_psum.append(raw)
+
+        old_sb = keep.tile([P, M], F32, name="old_sb", tag="words_then_old")
+        nc.sync.dma_start(old_sb[:], old)
+
+        grouped = [P, CHUNKS, Q // GROUP, GROUP]
+        scores = []
+        row_max = keep.tile([P, HALVES], F32, name="row_max", tag="max_then_signed")
+        raw_sbs, neg_bests = [], []
+        for h in range(HALVES):
+            raw_sb = keep.tile([P, CHUNKS, Q], F32, name="raw_sb%d" % h, tag=("worth_then_raw", "raw1")[h])
+            nc.scalar.copy(raw_sb[:], raw_psum[h][:])
+            neg_best = keep.tile([P, CHUNKS, Q // GROUP], F32, name="neg_best%d" % h, tag="best%d" % h)
+            nc.vector.tensor_reduce(
+                neg_best[:], raw_sb[:].rearrange("p c (v j) -> p c v j", j=GROUP), AX.X, ALU.max, negate=True
+            )
+            raw_sbs.append(raw_sb)
+            neg_bests.append(neg_best)
+        slot_worth = psum.tile([P, SLOTS], F32, name="slot_worth", tag="raw_then_worth")
+        for c in range(SLOTS // P):
+            nc.tensor.transpose(
+                slot_worth[:, c * P : (c + 1) * P], worth_cols[:, c : c + 1].to_broadcast([P, P]), ident[:]
+            )
+        for h in range(HALVES):
+            raw_sb, neg_best = raw_sbs[h], neg_bests[h]
+            shift = keep.tile([P, CHUNKS, Q], F32, name="shift%d" % h)
+            nc.vector.tensor_tensor(
+                shift[:].rearrange("p c (v j) -> p c v j", j=GROUP),
+                neg_best[:].unsqueeze(3).to_broadcast(grouped),
+                lam_row[:].rearrange("p (v j) -> p v j", j=GROUP).unsqueeze(1).to_broadcast(grouped),
+                ALU.mult,
+            )
+            score = psum.tile([P, HALF], F32, name="score%d" % h)
+            for c in range(CHUNKS):
+                cols = score[:, c * P : (c + 1) * P]
+                nc.tensor.matmul(cols, raw_sb[:, c, :], ident[:], is_transpose=True, start=True, stop=False)
+                nc.tensor.matmul(cols, shift[:, c, :], ident[:], is_transpose=True, start=False, stop=True)
+            scores.append(score)
+
+        wear0 = keep.tile([P, HALF], F32, name="wear0", tag="best0")
+        nc.vector.tensor_copy(wear0[:], wear_pool[:].indirect(half_list(0)))
+        wear1 = keep.tile([P, HALF], F32, name="wear1", tag="words1", align_bytes=64)
+        nc.scalar.activation(wear1[:], wear_pool[:].indirect(half_list(1)), ACT.Copy)
+        slot_wear = (wear0, wear1)
+        roots = {}
+        for h in (1, 0):
+            root = keep.tile([P, HALF], F32, name="root%d" % h)
+            nc.scalar.activation(root[:], slot_wear[h][:], ACT.Abs_reciprocal_sqrt, bias=1.0, scale=weary_col[:])
+            roots[h] = root
+
+        positive = keep.tile([P, HALVES, HALF], F32, name="positive", tag="best1")
+        for h in (1, 0):
+            nc.vector.tensor_scalar(positive[:, h, :], slot_wear[h][:], weary_col[:], -1.0, ALU.mult, ALU.is_gt)
+        for h in range(HALVES):
+            nc.vector.tensor_reduce(row_max[:, h : h + 1], scores[h][:], AX.X, ALU.max)
+        neg_max = keep.tile([P, 1], F32, name="neg_max")
+        nc.vector.tensor_reduce(neg_max[:], row_max[:], AX.X, ALU.max, negate=True)
+
+        signed = keep.tile([P, HALVES, HALF], F32, name="signed", tag="max_then_signed")
+        for h in range(HALVES):
+            nc.vector.scalar_tensor_tensor(signed[:, h, :], positive[:, h, :], -0.5, roots[h][:], ALU.add, ALU.mult)
+        half_inverses = []
+        for h in range(HALVES):
+            half_inverse = keep.tile([P, HALF], F32, name="half_inverse%d" % h)
+            nc.vector.tensor_tensor(half_inverse[:], signed[:, h, :], roots[h][:], ALU.mult)
+            half_inverses.append(half_inverse)
+
+        part_sums = keep.tile([P, HALVES], F32, name="part_sums")
+        parts = []
+        for h in range(HALVES):
+            expd = keep.tile([P, HALF], F32, name="expd%d" % h)
+            nc.scalar.activation(expd[:], scores[h][:], ACT.Exp, bias=neg_max[:])
+            part = keep.tile([P, HALF], F32, name="part%d" % h)
+            nc.vector.scalar_tensor_tensor(
+                part[:], expd[:], 1.0, half_inverses[h][:], ALU.mult, ALU.mult,
+                accum_out=part_sums[:, h : h + 1],
+            )
+            parts.append(part)
+
+        worthy = []
+        for h in range(HALVES):
+            prod = keep.tile([P, HALF], F32, name="worthy%d" % h)
+            nc.vector.tensor_tensor(prod[:], parts[h][:], slot_worth[:, half_cols(h)], ALU.mult)
+            worthy.append(prod)
+            if h == 0:
+                total = keep.tile([P, 1], F32, name="total")
+                nc.vector.tensor_reduce(total[:], part_sums[:], AX.X, ALU.add)
+        inv_total = keep.tile([P, 1], F32, name="inv_total")
+        nc.vector.reciprocal(inv_total[:], total[:])
+        factor = keep.tile([P, RUNS], F32, name="factor")
+        nc.scalar.activation(factor[:], inv_total[:].to_broadcast([P, RUNS]), ACT.Copy, scale=512.0)
+
+        run_sums = keep.tile([P, RUNS], F32, name="run_sums")
+        for h in range(HALVES):
+            nc.vector.tensor_reduce(
+                run_sums[:, half_cols(h, RUNS // HALVES)],
+                worthy[h][:].rearrange("p (g j) -> p g j", j=RUN),
+                AX.X,
+                ALU.add,
+            )
+        nc.vector.tensor_tensor(placed[:].indirect(run_list[:]), run_sums[:], factor[:], ALU.mult)
+
+        for h, queue in enumerate((nc.sync, nc.scalar)):
+            cols = half_cols(h, M // HALVES)
+            result = keep.tile([P, M // HALVES], F32, name="result%d" % h)
+            nc.vector.tensor_tensor(result[:], placed[:, cols], old_sb[:, cols], ALU.add)
+            queue.dma_start(out[:, cols], result[:])

@@ -51,6 +51,9 @@ def tile_attend_groupbest_wornout_pagesums_kernel(
                 keys_scales[0, 4 * quad : 4 * quad + 4, :].bitcast(I32),
             )
 
+        warm = keep.tile([P, 2], F32, name="warm")
+        nc.gpsimd.memset(warm[:, 0:1], 1.0)
+        nc.scalar.activation(warm[:, 1:2], warm[:, 0:1], ACT.Abs_reciprocal_sqrt)
         ident = keep.tile([P, P], F32, name="ident")
         make_identity(nc, ident[:])
         lam_col = keep.tile([P, 1], F32, name="lam_col")
@@ -166,6 +169,7 @@ def tile_attend_groupbest_wornout_pagesums_kernel(
             nc.scalar.activation(root[:], slot_wear[h][:], ACT.Abs_reciprocal_sqrt, bias=1.0, scale=weary_col[:])
             roots[h] = root
 
+        nc.scalar.activation(warm[:, 1:2], roots[0][:, 0:1], ACT.Exp)
         positive = keep.tile([P, HALVES, HALF], F32, name="positive", tag="best1")
         for h in (1, 0):
             nc.vector.tensor_scalar(positive[:, h, :], slot_wear[h][:], weary_col[:], -1.0, ALU.mult, ALU.is_gt)

@@ -1,7 +1,6 @@
 from contextlib import ExitStack
 
 import concourse.mybir as mybir
-from concourse.masks import make_identity
 
 D, T, SLOTS, Q, GROUP, RUN, RUNS, M = 512, 2048, 512, 128, 8, 8, 64, 512
 FLOPS = 2 * D * SLOTS * Q
@@ -24,6 +23,8 @@ HALVES = 2
 HALF = SLOTS // HALVES
 CHUNKS = HALF // P
 LANES = 16
+WORTH_ROW = 16
+VECTOR_CLEARS = 1280
 
 
 def tile_attend_groupbest_wornout_pagesums_kernel(
@@ -43,7 +44,12 @@ def tile_attend_groupbest_wornout_pagesums_kernel(
         def half_list(h):
             return slot_list[:, half_cols(h, HALF // LANES)]
 
-        scale_pool = keep.tile([P, T], U8, name="scale_pool")
+        run_list = keep.tile([P, RUNS // LANES], U16, name="run_list")
+        nc.sync.dma_start(run_list[:], offs2)
+        lam_col = keep.tile([P, 1], F32, name="lam_col")
+        with nc.allow_non_contiguous_dma(reason="one value a partition"):
+            nc.scalar.dma_start(lam_col[:], lam.rearrange("o q -> q o"))
+        scale_pool = keep.tile([P, T], U8, name="scale_pool", tag="words0", align_bytes=64)
         nc.gpsimd.memset(scale_pool[:].bitcast(I32), 0)
         for quad in range(4):
             nc.scalar.dma_start(
@@ -54,26 +60,33 @@ def tile_attend_groupbest_wornout_pagesums_kernel(
         warm = keep.tile([P, 2], F32, name="warm")
         nc.gpsimd.memset(warm[:, 0:1], 1.0)
         nc.scalar.activation(warm[:, 1:2], warm[:, 0:1], ACT.Abs_reciprocal_sqrt)
-        ident = keep.tile([P, P], F32, name="ident")
-        make_identity(nc, ident[:])
-        lam_col = keep.tile([P, 1], F32, name="lam_col")
-        with nc.allow_non_contiguous_dma(reason="one value a partition"):
-            nc.gpsimd.dma_start(lam_col[:], lam.rearrange("o q -> q o"))
-        weary_col = keep.tile([P, 1], F32, name="weary_col")
-        nc.gpsimd.dma_start(weary_col[:], weary)
-
-        query_raw = keep.tile([P, PACK, Q], F32, name="query_raw", tag="query_then_wear")
+        query_raw = keep.tile([P, PACK, Q], F32, name="query_raw")
         nc.sync.dma_start(query_raw[:], query.rearrange("(p j) q -> p j q", j=PACK))
-        word_pool = keep.tile([P, T], I32, name="word_pool", tag="words_then_old")
+        word_pool = keep.tile([P, T], I32, name="word_pool")
         nc.sync.dma_start(word_pool[:], keys_words[0].rearrange("p t r -> p (t r)").bitcast(I32))
 
-        worth_pool = keep.tile([P, T], F32, name="worth_pool")
-        nc.vector.memset(worth_pool[:].bitcast(I32), 0)
-        nc.sync.dma_start(worth_pool[0:1, :], worth[0:1, :])
+        worth_pool = keep.tile([P, T], F32, name="worth_pool", tag="worth_then_wear")
+        nc.vector.memset(worth_pool[:, :VECTOR_CLEARS].bitcast(I32), 0)
+        nc.gpsimd.memset(worth_pool[:, VECTOR_CLEARS:].bitcast(I32), 0)
+        nc.sync.dma_start(worth_pool[WORTH_ROW : WORTH_ROW + 1, :], worth[WORTH_ROW : WORTH_ROW + 1, :])
         placed = keep.tile([P, M], F32, name="placed")
         nc.vector.memset(placed[:].bitcast(I32), 0)
+        zeros = keep.tile([P, P], F32, name="zeros", tag="zeros_then_wear")
+        nc.gpsimd.memset(zeros[:], 0.0)
+        ident = keep.tile([P, P], F32, name="ident")
+        nc.gpsimd.affine_select(
+            out=ident[:],
+            in_=zeros[:],
+            compare_op=ALU.not_equal,
+            fill=1.0,
+            base=0,
+            pattern=[[-1, P]],
+            channel_multiplier=1,
+        )
+        wear_pool = keep.tile([P, T], F32, name="wear_pool", tag="zeros_then_wear")
+        nc.sync.dma_start(wear_pool[:], wear)
 
-        query_bf = keep.tile([P, Q, PACK], BF16, name="query_bf", align_bytes=64)
+        query_bf = keep.tile([P, Q, PACK], BF16, name="query_bf", tag="rounded_then_weary", align_bytes=64)
         nc.vector.tensor_copy(query_bf[:], query_raw[:].rearrange("p j q -> p q j"))
         query_words = keep.tile([P, Q], U32, name="query_words", align_bytes=64)
         query_scales = keep.tile([P, Q], U8, name="query_scales", align_bytes=64)
@@ -83,23 +96,16 @@ def tile_attend_groupbest_wornout_pagesums_kernel(
             in_=query_bf[:].rearrange("p q j -> p (q j)"),
         )
 
-        wear_pool = keep.tile([P, T], F32, name="wear_pool", tag="query_then_wear")
-        nc.sync.dma_start(wear_pool[:], wear)
-        run_list = keep.tile([P, RUNS // LANES], U16, name="run_list")
-        nc.sync.dma_start(run_list[:], offs2)
+        weary_col = keep.tile([P, 1], F32, name="weary_col", tag="rounded_then_weary", align_bytes=64)
+        nc.sync.dma_start(weary_col[:], weary)
 
         key_scales = keep.tile([P, SLOTS], U8, name="key_scales", align_bytes=64)
         nc.vector.tensor_copy(key_scales[:], scale_pool[:].indirect(slot_list[:]))
 
-        worth_listed = keep.tile([P, SLOTS], F32, name="worth_listed", tag="worth_then_raw")
+        worth_listed = keep.tile([P, SLOTS], F32, name="worth_listed")
         nc.scalar.activation(worth_listed[:], worth_pool[:].indirect(slot_list[:]), ACT.Copy)
-        turned = psum.tile([P, SLOTS // P, P], F32, name="turned", tag="turned_then_raw")
-        for c in range(SLOTS // P):
-            nc.tensor.transpose(turned[:, c, :], worth_listed[:, c * P : (c + 1) * P], ident[:])
-        worth_cols = keep.tile([P, SLOTS // P], F32, name="worth_cols")
-        nc.scalar.copy(worth_cols[:], turned[:, :, 0])
 
-        lam_row = psum.tile([P, Q], F32, name="lam_row")
+        lam_row = psum.tile([P, Q], F32, name="lam_row", tag="lam_then_worth")
         nc.tensor.transpose(lam_row[:], lam_col[:].to_broadcast([P, P]), ident[:])
 
         key_words, raw_psum = [], []
@@ -107,7 +113,7 @@ def tile_attend_groupbest_wornout_pagesums_kernel(
             words = keep.tile([P, HALF], U32, name="key_words%d" % h, tag="words%d" % h, align_bytes=64)
             nc.vector.tensor_copy(words[:], word_pool[:].bitcast(U32).indirect(half_list(h)))
             key_words.append(words)
-            raw = psum.tile([P, CHUNKS, Q], F32, name="raw%d" % h, tag=("raw_then_worth", "turned_then_raw")[h])
+            raw = psum.tile([P, CHUNKS, Q], F32, name="raw%d" % h)
             for c in range(CHUNKS):
                 first = h * HALF + c * P
                 nc.tensor.matmul_mx(
@@ -121,80 +127,78 @@ def tile_attend_groupbest_wornout_pagesums_kernel(
                 )
             raw_psum.append(raw)
 
-        old_sb = keep.tile([P, M], F32, name="old_sb", tag="words_then_old")
-        nc.sync.dma_start(old_sb[:], old)
 
         grouped = [P, CHUNKS, Q // GROUP, GROUP]
-        scores = []
-        row_max = keep.tile([P, HALVES], F32, name="row_max", tag="max_then_signed")
-        raw_sbs, neg_bests = [], []
+        neg_bests = []
         for h in range(HALVES):
-            raw_sb = keep.tile([P, CHUNKS, Q], F32, name="raw_sb%d" % h, tag=("worth_then_raw", "raw1")[h])
-            nc.scalar.copy(raw_sb[:], raw_psum[h][:])
-            neg_best = keep.tile([P, CHUNKS, Q // GROUP], F32, name="neg_best%d" % h, tag="best%d" % h)
+            neg_best = keep.tile([P, CHUNKS, Q // GROUP], F32, name="neg_best%d" % h)
             nc.vector.tensor_reduce(
-                neg_best[:], raw_sb[:].rearrange("p c (v j) -> p c v j", j=GROUP), AX.X, ALU.max, negate=True
+                neg_best[:], raw_psum[h][:].rearrange("p c (v j) -> p c v j", j=GROUP), AX.X, ALU.max, negate=True
             )
-            raw_sbs.append(raw_sb)
             neg_bests.append(neg_best)
-        slot_worth = psum.tile([P, SLOTS], F32, name="slot_worth", tag="raw_then_worth")
+        shifts = []
+        for h in range(HALVES):
+            shift = keep.tile([P, CHUNKS, Q], F32, name="shift%d" % h, tag="shift%d" % h)
+            nc.vector.tensor_tensor(
+                shift[:].rearrange("p c (v j) -> p c v j", j=GROUP),
+                neg_bests[h][:].unsqueeze(3).to_broadcast(grouped),
+                lam_row[:].rearrange("p (v j) -> p v j", j=GROUP).unsqueeze(1).to_broadcast(grouped),
+                ALU.mult,
+            )
+            shifts.append(shift)
+        scores = []
+        for h in range(HALVES):
+            by_slot = keep.tile([P, CHUNKS, Q], F32, name="by_slot%d" % h)
+            nc.vector.tensor_tensor(by_slot[:], raw_psum[h][:], shifts[h][:], ALU.add)
+            score = psum.tile([P, HALF], F32, name="score%d" % h, tag="score%d" % h)
+            for c in range(CHUNKS):
+                nc.tensor.transpose(score[:, c * P : (c + 1) * P], by_slot[:, c, :], ident[:])
+            scores.append(score)
+
+        slot_wear = keep.tile([P, SLOTS], F32, name="slot_wear", tag="worth_then_wear")
+        nc.scalar.activation(slot_wear[:], wear_pool[:].indirect(slot_list[:]), ACT.Copy)
+        old_sb = keep.tile([P, M], F32, name="old_sb", tag="zeros_then_wear")
+        nc.sync.dma_start(old_sb[:], old)
+        root = keep.tile([P, SLOTS], F32, name="root", tag="root_then_expd")
+        nc.scalar.activation(root[:], slot_wear[:], ACT.Abs_reciprocal_sqrt, bias=1.0, scale=weary_col[:])
+        abs_inverse = keep.tile([P, SLOTS], F32, name="abs_inverse")
+        nc.scalar.activation(abs_inverse[:], root[:], ACT.Square)
+        nc.scalar.activation(warm[:, 1:2], abs_inverse[:, 0:1], ACT.Exp)
+
+        positive = keep.tile([P, SLOTS], F32, name="positive", tag="shift1")
+        nc.vector.tensor_scalar(positive[:], slot_wear[:], weary_col[:], -1.0, ALU.mult, ALU.is_gt)
+        neg_scores = keep.tile([P, SLOTS], F32, name="neg_scores")
+        neg_max = None
+        for h in range(HALVES):
+            running = keep.tile([P, 1], F32, name="neg_max%d" % h)
+            nc.vector.tensor_scalar(
+                neg_scores[:, half_cols(h)], scores[h][:], -1.0, neg_max, ALU.mult, ALU.min, accum_out=running[:]
+            )
+            neg_max = running[:]
+        half_inverse = keep.tile([P, SLOTS], F32, name="half_inverse")
+        nc.vector.scalar_tensor_tensor(half_inverse[:], positive[:], -0.5, abs_inverse[:], ALU.add, ALU.mult)
+
+        turned = psum.tile([P, SLOTS // P, P], F32, name="turned", tag="score0")
+        for c in range(SLOTS // P):
+            nc.tensor.transpose(turned[:, c, :], worth_listed[:, c * P : (c + 1) * P], ident[:])
+        worth_cols = keep.tile([P, SLOTS // P], F32, name="worth_cols", tag="shift1")
+        nc.vector.tensor_copy(worth_cols[:], turned[:, :, WORTH_ROW])
+        slot_worth = psum.tile([P, SLOTS], F32, name="slot_worth", tag="lam_then_worth")
         for c in range(SLOTS // P):
             nc.tensor.transpose(
                 slot_worth[:, c * P : (c + 1) * P], worth_cols[:, c : c + 1].to_broadcast([P, P]), ident[:]
             )
-        for h in range(HALVES):
-            raw_sb, neg_best = raw_sbs[h], neg_bests[h]
-            shift = keep.tile([P, CHUNKS, Q], F32, name="shift%d" % h)
-            nc.vector.tensor_tensor(
-                shift[:].rearrange("p c (v j) -> p c v j", j=GROUP),
-                neg_best[:].unsqueeze(3).to_broadcast(grouped),
-                lam_row[:].rearrange("p (v j) -> p v j", j=GROUP).unsqueeze(1).to_broadcast(grouped),
-                ALU.mult,
-            )
-            score = psum.tile([P, HALF], F32, name="score%d" % h)
-            for c in range(CHUNKS):
-                cols = score[:, c * P : (c + 1) * P]
-                nc.tensor.matmul(cols, raw_sb[:, c, :], ident[:], is_transpose=True, start=True, stop=False)
-                nc.tensor.matmul(cols, shift[:, c, :], ident[:], is_transpose=True, start=False, stop=True)
-            scores.append(score)
-
-        wear0 = keep.tile([P, HALF], F32, name="wear0", tag="best0")
-        nc.vector.tensor_copy(wear0[:], wear_pool[:].indirect(half_list(0)))
-        wear1 = keep.tile([P, HALF], F32, name="wear1", tag="words1", align_bytes=64)
-        nc.scalar.activation(wear1[:], wear_pool[:].indirect(half_list(1)), ACT.Copy)
-        slot_wear = (wear0, wear1)
-        roots = {}
-        for h in (1, 0):
-            root = keep.tile([P, HALF], F32, name="root%d" % h)
-            nc.scalar.activation(root[:], slot_wear[h][:], ACT.Abs_reciprocal_sqrt, bias=1.0, scale=weary_col[:])
-            roots[h] = root
-
-        nc.scalar.activation(warm[:, 1:2], roots[0][:, 0:1], ACT.Exp)
-        positive = keep.tile([P, HALVES, HALF], F32, name="positive", tag="best1")
-        for h in (1, 0):
-            nc.vector.tensor_scalar(positive[:, h, :], slot_wear[h][:], weary_col[:], -1.0, ALU.mult, ALU.is_gt)
-        for h in range(HALVES):
-            nc.vector.tensor_reduce(row_max[:, h : h + 1], scores[h][:], AX.X, ALU.max)
-        neg_max = keep.tile([P, 1], F32, name="neg_max")
-        nc.vector.tensor_reduce(neg_max[:], row_max[:], AX.X, ALU.max, negate=True)
-
-        signed = keep.tile([P, HALVES, HALF], F32, name="signed", tag="max_then_signed")
-        for h in range(HALVES):
-            nc.vector.scalar_tensor_tensor(signed[:, h, :], positive[:, h, :], -0.5, roots[h][:], ALU.add, ALU.mult)
-        half_inverses = []
-        for h in range(HALVES):
-            half_inverse = keep.tile([P, HALF], F32, name="half_inverse%d" % h)
-            nc.vector.tensor_tensor(half_inverse[:], signed[:, h, :], roots[h][:], ALU.mult)
-            half_inverses.append(half_inverse)
 
         part_sums = keep.tile([P, HALVES], F32, name="part_sums")
         parts = []
+        expd = keep.tile([P, SLOTS], F32, name="expd", tag="root_then_expd")
         for h in range(HALVES):
-            expd = keep.tile([P, HALF], F32, name="expd%d" % h)
-            nc.scalar.activation(expd[:], scores[h][:], ACT.Exp, bias=neg_max[:])
+            nc.scalar.activation(
+                expd[:, half_cols(h)], neg_scores[:, half_cols(h)], ACT.Exp, bias=neg_max, scale=-1.0
+            )
             part = keep.tile([P, HALF], F32, name="part%d" % h)
             nc.vector.scalar_tensor_tensor(
-                part[:], expd[:], 1.0, half_inverses[h][:], ALU.mult, ALU.mult,
+                part[:], expd[:, half_cols(h)], 1.0, half_inverse[:, half_cols(h)], ALU.mult, ALU.mult,
                 accum_out=part_sums[:, h : h + 1],
             )
             parts.append(part)

@@ -49,7 +49,7 @@ def tile_attend_groupbest_wornout_pagesums_kernel(
         lam_col = keep.tile([P, 1], F32, name="lam_col")
         with nc.allow_non_contiguous_dma(reason="one value a partition"):
             nc.scalar.dma_start(lam_col[:], lam.rearrange("o q -> q o"))
-        scale_pool = keep.tile([P, T], U8, name="scale_pool", tag="words0", align_bytes=64)
+        scale_pool = keep.tile([P, T], U8, name="scale_pool")
         nc.gpsimd.memset(scale_pool[:].bitcast(I32), 0)
         for quad in range(4):
             nc.scalar.dma_start(
@@ -105,12 +105,12 @@ def tile_attend_groupbest_wornout_pagesums_kernel(
         worth_listed = keep.tile([P, SLOTS], F32, name="worth_listed")
         nc.scalar.activation(worth_listed[:], worth_pool[:].indirect(slot_list[:]), ACT.Copy)
 
-        lam_row = psum.tile([P, Q], F32, name="lam_row", tag="lam_then_worth")
+        lam_row = psum.tile([P, Q], F32, name="lam_row")
         nc.tensor.transpose(lam_row[:], lam_col[:].to_broadcast([P, P]), ident[:])
 
         key_words, raw_psum = [], []
         for h in range(HALVES):
-            words = keep.tile([P, HALF], U32, name="key_words%d" % h, tag="words%d" % h, align_bytes=64)
+            words = keep.tile([P, HALF], U32, name="key_words%d" % h, align_bytes=64)
             nc.vector.tensor_copy(words[:], word_pool[:].bitcast(U32).indirect(half_list(h)))
             key_words.append(words)
             raw = psum.tile([P, CHUNKS, Q], F32, name="raw%d" % h)
@@ -127,11 +127,14 @@ def tile_attend_groupbest_wornout_pagesums_kernel(
                 )
             raw_psum.append(raw)
 
+        turned = psum.tile([P, SLOTS // P, P], F32, name="turned")
+        for c in range(SLOTS // P):
+            nc.tensor.transpose(turned[:, c, :], worth_listed[:, c * P : (c + 1) * P], ident[:])
 
         grouped = [P, CHUNKS, Q // GROUP, GROUP]
         neg_bests = []
         for h in range(HALVES):
-            neg_best = keep.tile([P, CHUNKS, Q // GROUP], F32, name="neg_best%d" % h)
+            neg_best = keep.tile([P, CHUNKS, Q // GROUP], F32, name="neg_best%d" % h, tag="best%d" % h)
             nc.vector.tensor_reduce(
                 neg_best[:], raw_psum[h][:].rearrange("p c (v j) -> p c v j", j=GROUP), AX.X, ALU.max, negate=True
             )
@@ -146,6 +149,8 @@ def tile_attend_groupbest_wornout_pagesums_kernel(
                 ALU.mult,
             )
             shifts.append(shift)
+        worth_cols = keep.tile([P, SLOTS // P], F32, name="worth_cols", tag="best1")
+        nc.vector.tensor_copy(worth_cols[:], turned[:, :, WORTH_ROW])
         scores = []
         for h in range(HALVES):
             by_slot = keep.tile([P, CHUNKS, Q], F32, name="by_slot%d" % h)
@@ -163,7 +168,7 @@ def tile_attend_groupbest_wornout_pagesums_kernel(
         nc.scalar.activation(root[:], slot_wear[:], ACT.Abs_reciprocal_sqrt, bias=1.0, scale=weary_col[:])
         abs_inverse = keep.tile([P, SLOTS], F32, name="abs_inverse")
         nc.scalar.activation(abs_inverse[:], root[:], ACT.Square)
-        nc.scalar.activation(warm[:, 1:2], abs_inverse[:, 0:1], ACT.Exp)
+        nc.scalar.activation(warm[:, 1:2], abs_inverse[:, 0:1], ACT.Exp, scale=-1.0)
 
         positive = keep.tile([P, SLOTS], F32, name="positive", tag="shift1")
         nc.vector.tensor_scalar(positive[:], slot_wear[:], weary_col[:], -1.0, ALU.mult, ALU.is_gt)
@@ -178,12 +183,7 @@ def tile_attend_groupbest_wornout_pagesums_kernel(
         half_inverse = keep.tile([P, SLOTS], F32, name="half_inverse")
         nc.vector.scalar_tensor_tensor(half_inverse[:], positive[:], -0.5, abs_inverse[:], ALU.add, ALU.mult)
 
-        turned = psum.tile([P, SLOTS // P, P], F32, name="turned", tag="score0")
-        for c in range(SLOTS // P):
-            nc.tensor.transpose(turned[:, c, :], worth_listed[:, c * P : (c + 1) * P], ident[:])
-        worth_cols = keep.tile([P, SLOTS // P], F32, name="worth_cols", tag="shift1")
-        nc.vector.tensor_copy(worth_cols[:], turned[:, :, WORTH_ROW])
-        slot_worth = psum.tile([P, SLOTS], F32, name="slot_worth", tag="lam_then_worth")
+        slot_worth = psum.tile([P, SLOTS], F32, name="slot_worth", tag="score0")
         for c in range(SLOTS // P):
             nc.tensor.transpose(
                 slot_worth[:, c * P : (c + 1) * P], worth_cols[:, c : c + 1].to_broadcast([P, P]), ident[:]

from contextlib import ExitStack

import concourse.mybir as mybir

D, T, SLOTS, Q, GROUP, RUN, RUNS, M = 512, 2048, 512, 128, 8, 8, 64, 512
FLOPS = 2 * D * SLOTS * Q
BYTES = 4 * (D * Q + 128 * T + 4 * T + Q + Q * T + Q + T + 2 * Q * M) + 2 * 128 * (32 + 4)

F32 = mybir.dt.float32
BF16 = mybir.dt.bfloat16
I32 = mybir.dt.int32
U32 = mybir.dt.uint32
U16 = mybir.dt.uint16
U8 = mybir.dt.uint8
FP8X4 = mybir.dt.float8_e4m3fn_x4
ALU = mybir.AluOpType
ACT = mybir.ActivationFunctionType
AX = mybir.AxisListType

P = 128
PACK = 4
HALVES = 2
HALF = SLOTS // HALVES
CHUNKS = HALF // P
LANES = 16
WORTH_ROW = 16
VECTOR_CLEARS = 1280


def tile_attend_groupbest_wornout_pagesums_kernel(
    tc, query, keys_words, keys_scales, lam, wear, weary, worth, old, offs, offs2, out
):
    nc = tc.nc
    with ExitStack() as ctx:
        keep = ctx.enter_context(tc.tile_pool(name="keep", bufs=1))
        psum = ctx.enter_context(tc.psum_pool(name="psum", bufs=1))

        def half_cols(h, width=HALF):
            return slice(h * width, (h + 1) * width)

        slot_list = keep.tile([P, SLOTS // LANES], U16, name="slot_list")
        nc.sync.dma_start(slot_list[:], offs)

        def half_list(h):
            return slot_list[:, half_cols(h, HALF // LANES)]

        run_list = keep.tile([P, RUNS // LANES], U16, name="run_list")
        nc.sync.dma_start(run_list[:], offs2)
        lam_col = keep.tile([P, 1], F32, name="lam_col")
        with nc.allow_non_contiguous_dma(reason="one value a partition"):
            nc.scalar.dma_start(lam_col[:], lam.rearrange("o q -> q o"))
        scale_pool = keep.tile([P, T], U8, name="scale_pool")
        nc.gpsimd.memset(scale_pool[:].bitcast(I32), 0)
        for quad in range(4):
            nc.scalar.dma_start(
                scale_pool[32 * quad : 32 * quad + 4, :].bitcast(I32),
                keys_scales[0, 4 * quad : 4 * quad + 4, :].bitcast(I32),
            )

        warm = keep.tile([P, 2], F32, name="warm")
        nc.gpsimd.memset(warm[:, 0:1], 1.0)
        nc.scalar.activation(warm[:, 1:2], warm[:, 0:1], ACT.Abs_reciprocal_sqrt)
        query_raw = keep.tile([P, PACK, Q], F32, name="query_raw")
        nc.sync.dma_start(query_raw[:], query.rearrange("(p j) q -> p j q", j=PACK))
        word_pool = keep.tile([P, T], I32, name="word_pool")
        nc.sync.dma_start(word_pool[:], keys_words[0].rearrange("p t r -> p (t r)").bitcast(I32))

        worth_pool = keep.tile([P, T], F32, name="worth_pool", tag="worth_then_wear")
        nc.vector.memset(worth_pool[:, :VECTOR_CLEARS].bitcast(I32), 0)
        nc.gpsimd.memset(worth_pool[:, VECTOR_CLEARS:].bitcast(I32), 0)
        nc.sync.dma_start(worth_pool[WORTH_ROW : WORTH_ROW + 1, :], worth[WORTH_ROW : WORTH_ROW + 1, :])
        placed = keep.tile([P, M], F32, name="placed")
        nc.vector.memset(placed[:].bitcast(I32), 0)
        zeros = keep.tile([P, P], F32, name="zeros", tag="zeros_then_wear")
        nc.gpsimd.memset(zeros[:], 0.0)
        ident = keep.tile([P, P], F32, name="ident")
        nc.gpsimd.affine_select(
            out=ident[:],
            in_=zeros[:],
            compare_op=ALU.not_equal,
            fill=1.0,
            base=0,
            pattern=[[-1, P]],
            channel_multiplier=1,
        )
        wear_pool = keep.tile([P, T], F32, name="wear_pool", tag="zeros_then_wear")
        nc.sync.dma_start(wear_pool[:], wear)

        query_bf = keep.tile([P, Q, PACK], BF16, name="query_bf", tag="rounded_then_weary", align_bytes=64)
        nc.vector.tensor_copy(query_bf[:], query_raw[:].rearrange("p j q -> p q j"))
        query_words = keep.tile([P, Q], U32, name="query_words", align_bytes=64)
        query_scales = keep.tile([P, Q], U8, name="query_scales", align_bytes=64)
        nc.vector.quantize_mx(
            out=query_words[:].bitcast(FP8X4),
            scales=query_scales[:],
            in_=query_bf[:].rearrange("p q j -> p (q j)"),
        )

        weary_col = keep.tile([P, 1], F32, name="weary_col", tag="rounded_then_weary", align_bytes=64)
        nc.sync.dma_start(weary_col[:], weary)

        key_scales = keep.tile([P, SLOTS], U8, name="key_scales", align_bytes=64)
        nc.vector.tensor_copy(key_scales[:], scale_pool[:].indirect(slot_list[:]))

        worth_listed = keep.tile([P, SLOTS], F32, name="worth_listed")
        nc.scalar.activation(worth_listed[:], worth_pool[:].indirect(slot_list[:]), ACT.Copy)

        lam_row = psum.tile([P, Q], F32, name="lam_row")
        nc.tensor.transpose(lam_row[:], lam_col[:].to_broadcast([P, P]), ident[:])

        key_words, raw_psum = [], []
        for h in range(HALVES):
            words = keep.tile([P, HALF], U32, name="key_words%d" % h, align_bytes=64)
            nc.vector.tensor_copy(words[:], word_pool[:].bitcast(U32).indirect(half_list(h)))
            key_words.append(words)
            raw = psum.tile([P, CHUNKS, Q], F32, name="raw%d" % h)
            for c in range(CHUNKS):
                first = h * HALF + c * P
                nc.tensor.matmul_mx(
                    out=raw[:, c, :],
                    lhsT=words[:, c * P : (c + 1) * P].bitcast(FP8X4),
                    lhsT_scale=key_scales[:, first : first + P],
                    rhs=query_words[:].bitcast(FP8X4),
                    rhs_scale=query_scales[:],
                    start=True,
                    stop=True,
                )
            raw_psum.append(raw)

        turned = psum.tile([P, SLOTS // P, P], F32, name="turned")
        for c in range(SLOTS // P):
            nc.tensor.transpose(turned[:, c, :], worth_listed[:, c * P : (c + 1) * P], ident[:])

        grouped = [P, CHUNKS, Q // GROUP, GROUP]
        neg_bests = []
        for h in range(HALVES):
            neg_best = keep.tile([P, CHUNKS, Q // GROUP], F32, name="neg_best%d" % h, tag="best%d" % h)
            nc.vector.tensor_reduce(
                neg_best[:], raw_psum[h][:].rearrange("p c (v j) -> p c v j", j=GROUP), AX.X, ALU.max, negate=True
            )
            neg_bests.append(neg_best)
        shifts = []
        for h in range(HALVES):
            shift = keep.tile([P, CHUNKS, Q], F32, name="shift%d" % h, tag="shift%d" % h)
            nc.vector.tensor_tensor(
                shift[:].rearrange("p c (v j) -> p c v j", j=GROUP),
                neg_bests[h][:].unsqueeze(3).to_broadcast(grouped),
                lam_row[:].rearrange("p (v j) -> p v j", j=GROUP).unsqueeze(1).to_broadcast(grouped),
                ALU.mult,
            )
            shifts.append(shift)
        worth_cols = keep.tile([P, SLOTS // P], F32, name="worth_cols", tag="best1")
        nc.vector.tensor_copy(worth_cols[:], turned[:, :, WORTH_ROW])
        scores = []
        for h in range(HALVES):
            by_slot = keep.tile([P, CHUNKS, Q], F32, name="by_slot%d" % h)
            nc.vector.tensor_tensor(by_slot[:], raw_psum[h][:], shifts[h][:], ALU.add)
            score = psum.tile([P, HALF], F32, name="score%d" % h, tag="score%d" % h)
            for c in range(CHUNKS):
                nc.tensor.transpose(score[:, c * P : (c + 1) * P], by_slot[:, c, :], ident[:])
            scores.append(score)

        slot_wear = keep.tile([P, SLOTS], F32, name="slot_wear", tag="worth_then_wear")
        nc.scalar.activation(slot_wear[:], wear_pool[:].indirect(slot_list[:]), ACT.Copy)
        old_sb = keep.tile([P, M], F32, name="old_sb", tag="zeros_then_wear")
        nc.sync.dma_start(old_sb[:], old)
        root = keep.tile([P, SLOTS], F32, name="root", tag="root_then_expd")
        nc.scalar.activation(root[:], slot_wear[:], ACT.Abs_reciprocal_sqrt, bias=1.0, scale=weary_col[:])
        abs_inverse = keep.tile([P, SLOTS], F32, name="abs_inverse")
        nc.scalar.activation(abs_inverse[:], root[:], ACT.Square)
        nc.scalar.activation(warm[:, 1:2], abs_inverse[:, 0:1], ACT.Exp, scale=-1.0)

        positive = keep.tile([P, SLOTS], F32, name="positive", tag="shift1")
        nc.vector.tensor_scalar(positive[:], slot_wear[:], weary_col[:], -1.0, ALU.mult, ALU.is_gt)
        neg_scores = keep.tile([P, SLOTS], F32, name="neg_scores")
        neg_max = None
        for h in range(HALVES):
            running = keep.tile([P, 1], F32, name="neg_max%d" % h)
            nc.vector.tensor_scalar(
                neg_scores[:, half_cols(h)], scores[h][:], -1.0, neg_max, ALU.mult, ALU.min, accum_out=running[:]
            )
            neg_max = running[:]
        half_inverse = keep.tile([P, SLOTS], F32, name="half_inverse")
        nc.vector.scalar_tensor_tensor(half_inverse[:], positive[:], -0.5, abs_inverse[:], ALU.add, ALU.mult)

        slot_worth = psum.tile([P, SLOTS], F32, name="slot_worth", tag="score0")
        for c in range(SLOTS // P):
            nc.tensor.transpose(
                slot_worth[:, c * P : (c + 1) * P], worth_cols[:, c : c + 1].to_broadcast([P, P]), ident[:]
            )

        part_sums = keep.tile([P, HALVES], F32, name="part_sums")
        parts = []
        expd = keep.tile([P, SLOTS], F32, name="expd", tag="root_then_expd")
        for h in range(HALVES):
            nc.scalar.activation(
                expd[:, half_cols(h)], neg_scores[:, half_cols(h)], ACT.Exp, bias=neg_max, scale=-1.0
            )
            part = keep.tile([P, HALF], F32, name="part%d" % h)
            nc.vector.scalar_tensor_tensor(
                part[:], expd[:, half_cols(h)], 1.0, half_inverse[:, half_cols(h)], ALU.mult, ALU.mult,
                accum_out=part_sums[:, h : h + 1],
            )
            parts.append(part)

        worthy = []
        for h in range(HALVES):
            prod = keep.tile([P, HALF], F32, name="worthy%d" % h)
            nc.vector.tensor_tensor(prod[:], parts[h][:], slot_worth[:, half_cols(h)], ALU.mult)
            worthy.append(prod)
            if h == 0:
                total = keep.tile([P, 1], F32, name="total")
                nc.vector.tensor_reduce(total[:], part_sums[:], AX.X, ALU.add)
        inv_total = keep.tile([P, 1], F32, name="inv_total")
        nc.vector.reciprocal(inv_total[:], total[:])
        factor = keep.tile([P, RUNS], F32, name="factor")
        nc.scalar.activation(factor[:], inv_total[:].to_broadcast([P, RUNS]), ACT.Copy, scale=512.0)

        run_sums = keep.tile([P, RUNS], F32, name="run_sums")
        for h in range(HALVES):
            nc.vector.tensor_reduce(
                run_sums[:, half_cols(h, RUNS // HALVES)],
                worthy[h][:].rearrange("p (g j) -> p g j", j=RUN),
                AX.X,
                ALU.add,
            )
        nc.vector.tensor_tensor(placed[:].indirect(run_list[:]), run_sums[:], factor[:], ALU.mult)

        for h, queue in enumerate((nc.sync, nc.scalar)):
            cols = half_cols(h, M // HALVES)
            result = keep.tile([P, M // HALVES], F32, name="result%d" % h)
            nc.vector.tensor_tensor(result[:], placed[:, cols], old_sb[:, cols], ALU.add)
            queue.dma_start(out[:, cols], result[:])
